import numpy as np
import ml_dtypes


def mxq(x, axis, fmt="e4m3"):
    dtype, down = {"e4m3": (ml_dtypes.float8_e4m3fn, 7), "e5m2": (ml_dtypes.float8_e5m2, 14)}[fmt]
    v = np.moveaxis(np.asarray(x, np.float32).astype(ml_dtypes.bfloat16).astype(np.float64), axis, -1)
    blocks = v.reshape(v.shape[:-1] + (-1, 32))
    amax = np.abs(blocks).max(-1, keepdims=True)
    byte = np.maximum(np.where(amax > 0, np.frexp(amax)[1] - 1 + 127, 0) - down, 1)
    scale = np.exp2(byte - 127.0)
    codes = (blocks / scale).astype(np.float32).astype(dtype).astype(np.float64)
    return np.moveaxis((codes * scale).reshape(v.shape), -1, axis)


WIDE = False


def mx_kscale(k):
    if not WIDE:
        return np.ones(k)
    levels = np.array([30, -30])
    if k % 512:
        return np.exp2(np.random.permutation(np.resize(levels, k // 32))).repeat(32)
    a = np.empty((k // 512, 16))
    for p in range(k // 512):
        a[p, :8] = np.random.permutation(np.resize(levels, 8))
        for g in range(8):
            far = levels[np.abs(levels - a[p, g]) >= 10]
            a[p, g + 8] = far[np.random.randint(len(far))]
    return np.exp2(a.ravel()).repeat(32)


def f64(x):
    return np.asarray(x).astype(np.float64)


def striped(idx):
    return np.tile(idx.reshape(-1, 16).T, (8, 1)).astype(np.uint16)


def unstriped(offs):
    return offs[:16].T.reshape(-1).astype(np.int64)


E2M1 = np.array([0.0, 0.5, 1.0, 1.5, 2.0, 3.0, 4.0, 6.0, -0.0, -0.5, -1.0, -1.5, -2.0, -3.0, -4.0, -6.0])


def pack_weight(w, fmt):
    k, n = w.shape
    w = f64(np.asarray(w, np.float32).astype(ml_dtypes.bfloat16)).reshape(k // 32, 32, n)
    amax = np.abs(w).max(1)
    if fmt == "e4m3":
        byte = np.frexp(amax)[1] - 1 + 127 - 7
    elif fmt == "e5m2":
        byte = np.frexp(amax)[1] - 1 + 127 - 14
    else:
        mant, ex = np.frexp(amax / 6.0)
        byte = np.where(mant > 0.5, ex, ex - 1) + 127
    byte = np.clip(np.where(amax > 0, byte, 1), 1, 254)
    scaled = (w * np.exp2(127.0 - byte)[:, None, :]).reshape(k, n).astype(np.float32)
    by_word = np.ascontiguousarray(scaled.reshape(k // 512, 128, 4, n).transpose(0, 1, 3, 2))
    if fmt == "e4m3":
        words = by_word.astype(ml_dtypes.float8_e4m3fn).view(np.uint8)
    elif fmt == "e5m2":
        words = by_word.astype(ml_dtypes.float8_e5m2).view(np.uint8)
    else:
        c = by_word.astype(ml_dtypes.float4_e2m1fn).view(np.uint8) & 0xF
        words = (c[..., 0::2] | (c[..., 1::2] << 4)).reshape(k // 512, 128, 2 * n)
    return np.ascontiguousarray(words), np.ascontiguousarray(byte.astype(np.uint8).reshape(k // 512, 16, n))


def unpack_weight(words, scales, fmt):
    g, _, n = scales.shape
    words = np.ascontiguousarray(words).reshape(g, 128, n, -1)
    if fmt == "e4m3":
        vals = words.view(ml_dtypes.float8_e4m3fn).astype(np.float64)
    elif fmt == "e5m2":
        vals = words.view(ml_dtypes.float8_e5m2).astype(np.float64)
    else:
        nib = np.empty((g, 128, n, 4), np.uint8)
        nib[..., 0::2] = words & 0xF
        nib[..., 1::2] = words >> 4
        vals = E2M1[nib]
    vals = vals * np.repeat(np.exp2(scales.astype(np.float64) - 127.0), 8, axis=1)[..., None]
    return vals.transpose(0, 1, 3, 2).reshape(g * 512, n)


K, T, E, C, N = 256, 1536, 2, 512, 1024


def by_expert(wq, xq):
    return np.concatenate([wq[e].T @ xq[:, e * C:(e + 1) * C] for e in range(E)], axis=1)


def setup_inputs():
    n = np.random.standard_normal
    s = mx_kscale(N)[:, None]
    dy = pack_weight(n((N, T)) * s, "e5m2")
    return {
        "dy_words": dy[0],
        "dy_scales": dy[1],
        "w": (n((E + 1, N, K)) / np.sqrt(N) / s[None]).astype(np.float32),
        "gate": np.tile(np.random.uniform(0.2, 1.0, E * C), (K, 1)).astype(np.float32),
        "offs": striped(np.random.permutation(T)[:E * C]),
    }


def reference(dy_words, dy_scales, w, gate, offs):
    idx = unstriped(offs)
    gq = unpack_weight(dy_words, dy_scales, "e5m2")[:, idx]
    wq = mxq(f64(w), 1, "e4m3")
    ds = wq[E].T @ unpack_weight(dy_words, dy_scales, "e5m2")
    dx = f64(gate) * by_expert(wq, gq)
    ds[:, idx] += dx
    return ds

@@ -1,0 +1,188 @@
+from contextlib import ExitStack
+
+import concourse.mybir as mybir
+from concourse.masks import make_identity
+
+K, T, E, C, N = 256, 1536, 2, 512, 1024
+S = E * C
+P = 128
+PACK = 4
+PASSES = N // (P * PACK)
+BANK = 512
+QUADS = 4
+SHIFT = 16
+
+FLOPS = 2 * N * K * (S + T)
+BYTES = N * T + N * T // 32 + 4 * (E + 1) * N * K + 4 * S + 2 * P * (S // 16) + 4 * K * T
+
+F32 = mybir.dt.float32
+BF16 = mybir.dt.bfloat16
+I32 = mybir.dt.int32
+U32 = mybir.dt.uint32
+U16 = mybir.dt.uint16
+U8 = mybir.dt.uint8
+E4M3 = mybir.dt.float8_e4m3fn_x4
+E5M2 = mybir.dt.float8_e5m2_x4
+MULT = mybir.AluOpType.mult
+ADD = mybir.AluOpType.add
+
+
+def tile_moe_bds_lin_none_kernel(tc, dy_words, dy_scales, w, gate, offs, out):
+    nc = tc.nc
+    with ExitStack() as ctx:
+        keep = ctx.enter_context(tc.tile_pool(name="keep", bufs=1))
+        psum = ctx.enter_context(tc.psum_pool(name="psum", bufs=1))
+
+        offsets = keep.tile([P, S // 16], U16, name="offsets")
+        nc.sync.dma_start(offsets[:], offs)
+
+        def slot_offsets(e):
+            return offsets[:, e * (C // 16) : (e + 1) * (C // 16)]
+
+        token_scales = keep.tile([P, T], U8, name="token_scales", align_bytes=64)
+        nc.vector.memset(token_scales[:].bitcast(I32), 0)
+        scale_rows = dy_scales.bitcast(I32).rearrange("o (q r) c -> r q o c", r=4)
+        for r in range(4):
+            nc.scalar.dma_start(token_scales[:].bitcast(I32)[r:P:SHIFT, :], scale_rows[r])
+
+        token_words = []
+        for o in range(PASSES):
+            words = keep.tile([P, T], I32, name="token_words%d" % o, align_bytes=64)
+            nc.sync.dma_start(words[:], dy_words[o].rearrange("p t d -> p (t d)").bitcast(I32))
+            token_words.append(words)
+
+        slot_scales1 = keep.tile([P, S], U8, name="slot_scales1", align_bytes=64)
+        nc.vector.memset(slot_scales1[:].bitcast(I32), 0)
+        token_scales1 = keep.tile([P, T], U8, name="token_scales1", align_bytes=64)
+        nc.vector.memset(token_scales1[:].bitcast(I32), 0)
+        windows = [keep.tile([P, T], F32, name="window%d" % b) for b in range(2)]
+        nc.vector.memset(windows[0][:], 0.0)
+        nc.scalar.copy(windows[1][:], windows[0][:])
+        ident = keep.tile([P, P], F32, name="ident")
+        make_identity(nc, ident[:])
+
+        w_raw = {}
+
+        def load_w(e, o):
+            raw = keep.tile([P, PACK, K], F32, name="w_raw", tag="w_raw%d%d" % (e, o))
+            nc.sync.dma_start(raw[:], w[e, o * 512 : (o + 1) * 512, :].rearrange("(p j) k -> p j k", j=PACK))
+            w_raw[e, o] = raw
+
+        gates = {}
+
+        def load_gate(e):
+            g = keep.tile([P, C], F32, name="gate%d" % e)
+            nc.sync.dma_start(g[:], gate[0:P, e * C : (e + 1) * C])
+            gates[e] = g
+
+        for e in range(E):
+            for o in range(PASSES):
+                load_w(e, o)
+        load_gate(0)
+        for o in range(PASSES):
+            load_w(E, o)
+        load_gate(1)
+        for r in range(4):
+            nc.sync.dma_start(token_scales1[:].bitcast(I32)[r:P:32, :], scale_rows[r, :, 1, :])
+
+        slot_scales0 = keep.tile([P, S], U8, name="slot_scales0", align_bytes=64)
+        nc.vector.tensor_copy(slot_scales0[:], token_scales[:].indirect(offsets[:]))
+        for r in range(4):
+            nc.scalar.dma_start(
+                slot_scales1[:].bitcast(I32)[r:P:32, :], slot_scales0[:].bitcast(I32)[SHIFT + r : P : 32, :]
+            )
+        slot_scales = [slot_scales0, slot_scales1]
+        slot_words0 = keep.tile([P, S], U32, name="slot_words0", align_bytes=64)
+        nc.vector.tensor_copy(slot_words0[:], token_words[0][:].bitcast(U32).indirect(offsets[:]))
+        slot_words = {(0, e): slot_words0[:, e * C : (e + 1) * C] for e in range(E)}
+
+        def gather_pass1(e, tag):
+            words = keep.tile([P, C], U32, name="slot_words1", tag=tag, align_bytes=64)
+            nc.vector.tensor_copy(words[:], token_words[1][:].bitcast(U32).indirect(slot_offsets(e)))
+            slot_words[1, e] = words[:]
+
+        codes = {}
+        scales = {}
+
+        def quantize_w(e, o):
+            grouped = keep.tile([P, K, PACK], BF16, name="w_grouped", tag="w_grouped%d%d" % (e, o), align_bytes=64)
+            nc.scalar.copy(
+                grouped[:].rearrange("p (c i) j -> p c j i", i=4),
+                w_raw[e, o][:].rearrange("p j (c i) -> p c j i", i=4),
+            )
+            codes[e, o] = keep.tile([P, K], U32, name="w_codes%d%d" % (e, o), align_bytes=64)
+            scales[e, o] = keep.tile([P, K], U8, name="w_scales%d%d" % (e, o), align_bytes=64)
+            nc.vector.quantize_mx(
+                out=codes[e, o][:].bitcast(E4M3), scales=scales[e, o][:], in_=grouped[:].rearrange("p k j -> p (k j)")
+            )
+
+        def product(acc, e, b, moving, moving_scales):
+            cols = slice(b * P, (b + 1) * P)
+            for o in range(PASSES):
+                nc.tensor.matmul_mx(
+                    out=acc,
+                    lhsT=codes[e, o][:, cols].bitcast(E4M3),
+                    lhsT_scale=scales[e, o][:, cols],
+                    rhs=moving[o].bitcast(E5M2),
+                    rhs_scale=moving_scales[o],
+                    start=(o == 0),
+                    stop=(o == PASSES - 1),
+                )
+
+        def routed(e, b, staged):
+            acc = psum.tile([P, C], F32, name="dx", tag="ring2", bufs=2)
+            cols = slice(e * C, (e + 1) * C)
+            product(acc[:], e, b, [slot_words[o, e] for o in range(PASSES)], [s[:, cols] for s in slot_scales])
+            nc.scalar.copy(staged, acc[:])
+            nc.vector.tensor_tensor(windows[b][:].indirect(slot_offsets(e)), staged, gates[e][:], MULT)
+
+        def shared(acc, b, c):
+            cols = slice(c * BANK, (c + 1) * BANK)
+            product(acc, E, b, [t[:, cols] for t in token_words], [token_scales[:, cols], token_scales1[:, cols]])
+
+        gather_pass1(0, "slot_words10")
+        for o in range(PASSES):
+            quantize_w(0, o)
+        gather_pass1(1, "w_grouped01")
+        for o in range(PASSES):
+            quantize_w(1, o)
+        staged_a = keep.tile([P, 2 * C], F32, name="staged_a", tag="w_raw11")
+        routed(0, 0, staged_a[:, 0:C])
+        for o in range(PASSES):
+            quantize_w(E, o)
+        staged_b = keep.tile([P, 2 * C], F32, name="staged_b", tag="w_raw21")
+        routed(1, 0, staged_b[:, 0:C])
+        routed(0, 1, staged_b[:, C : 2 * C])
+        routed(1, 1, staged_a[:, C : 2 * C])
+
+        ds0 = keep.tile([P, T], F32, name="ds0")
+        for c in range(T // BANK):
+            acc = psum.tile([P, BANK], F32, name="ds0_acc", tag="ring3", bufs=3)
+            shared(acc[:], 0, c)
+            nc.scalar.copy(ds0[:, c * BANK : (c + 1) * BANK], acc[:])
+        ds1 = []
+        for c in range(T // BANK):
+            acc = psum.tile([P, BANK], F32, name="ds1_acc%d" % c)
+            shared(acc[:], 1, c)
+            ds1.append(acc)
+        for c in range(T // BANK):
+            turned = psum.tile([P, BANK], F32, name="turned", tag="ring3", bufs=3)
+            for j in range(BANK // P):
+                cols = slice(c * BANK + j * P, c * BANK + (j + 1) * P)
+                dst = turned[:, j * P : (j + 1) * P]
+                nc.tensor.matmul(dst, ds0[:, cols], ident[:], start=True, stop=False, is_transpose=True)
+                nc.tensor.matmul(dst, windows[0][:, cols], ident[:], start=False, stop=True, is_transpose=True)
+            sums = keep.tile([P, BANK], F32, name="sums%d" % c)
+            nc.scalar.copy(sums[:], turned[:])
+            back = psum.tile([P, BANK], F32, name="back", tag="ring2", bufs=2)
+            for j in range(BANK // P):
+                nc.tensor.transpose(back[:, j * P : (j + 1) * P], sums[:, j * P : (j + 1) * P], ident[:])
+            result = keep.tile([P, BANK], F32, name="result0_%d" % c)
+            nc.scalar.copy(result[:], back[:])
+            nc.sync.dma_start(out[0:P, c * BANK : (c + 1) * BANK], result[:])
+
+        for c in range(T // BANK):
+            cols = slice(c * BANK, (c + 1) * BANK)
+            result = keep.tile([P, BANK], F32, name="result1_%d" % c)
+            nc.vector.tensor_tensor(result[:], ds1[c][:], windows[1][:, cols], ADD)
+            nc.sync.dma_start(out[P : 2 * P, cols], result[:])

@@ -10,7 +10,8 @@ PACK = 4
 PASSES = N // (P * PACK)
 BANK = 512
 QUADS = 4
-SHIFT = 16
+FIRST = 24
+MOVED = 100
 
 FLOPS = 2 * N * K * (S + T)
 BYTES = N * T + N * T // 32 + 4 * (E + 1) * N * K + 4 * S + 2 * P * (S // 16) + 4 * K * T
@@ -39,11 +40,13 @@ def tile_moe_bds_lin_none_kernel(tc, dy_words, dy_scales, w, gate, offs, out):
         def slot_offsets(e):
             return offsets[:, e * (C // 16) : (e + 1) * (C // 16)]
 
-        token_scales = keep.tile([P, T], U8, name="token_scales", align_bytes=64)
-        nc.vector.memset(token_scales[:].bitcast(I32), 0)
-        scale_rows = dy_scales.bitcast(I32).rearrange("o (q r) c -> r q o c", r=4)
-        for r in range(4):
-            nc.scalar.dma_start(token_scales[:].bitcast(I32)[r:P:SHIFT, :], scale_rows[r])
+        scale_window = keep.tile([P, T], U8, name="scale_window", align_bytes=64)
+        for q in range(QUADS):
+            nc.sync.dma_start(
+                scale_window[:].bitcast(I32)[32 * q + FIRST : 32 * (q + 1), :],
+                dy_scales.bitcast(I32)[:, 4 * q : 4 * (q + 1), :],
+            )
+            nc.vector.memset(scale_window[:].bitcast(I32)[32 * q : 32 * q + FIRST, :], 0)
 
         token_words = []
         for o in range(PASSES):
@@ -51,47 +54,50 @@ def tile_moe_bds_lin_none_kernel(tc, dy_words, dy_scales, w, gate, offs, out):
             nc.sync.dma_start(words[:], dy_words[o].rearrange("p t d -> p (t d)").bitcast(I32))
             token_words.append(words)
 
-        slot_scales1 = keep.tile([P, S], U8, name="slot_scales1", align_bytes=64)
-        nc.vector.memset(slot_scales1[:].bitcast(I32), 0)
-        token_scales1 = keep.tile([P, T], U8, name="token_scales1", align_bytes=64)
-        nc.vector.memset(token_scales1[:].bitcast(I32), 0)
+        slot_scales = keep.tile([P, PASSES, S], U8, name="slot_scales", align_bytes=64)
+        nc.vector.memset(slot_scales[:].bitcast(I32), 0)
+        token_scales = keep.tile([P, PASSES, T], U8, name="token_scales", align_bytes=64)
+        nc.vector.memset(token_scales[:].bitcast(I32), 0)
+
+        def move_scales(queue, planes, rows):
+            for o in range(PASSES):
+                first = FIRST + 4 * o
+                queue.dma_start(planes[:].bitcast(I32)[0:MOVED, o, :], rows[:].bitcast(I32)[first : first + MOVED, :])
+
         windows = [keep.tile([P, T], F32, name="window%d" % b) for b in range(2)]
-        nc.vector.memset(windows[0][:], 0.0)
-        nc.scalar.copy(windows[1][:], windows[0][:])
+        zeros = keep.tile([P, 64], F32, name="zeros")
+        nc.gpsimd.memset(zeros[:], 0.0)
+        for window in windows:
+            nc.scalar.copy(
+                window[:].rearrange("p (a b) -> p a b", b=64), zeros[:].unsqueeze(1).to_broadcast([P, T // 64, 64])
+            )
         ident = keep.tile([P, P], F32, name="ident")
         make_identity(nc, ident[:])
 
         w_raw = {}
 
         def load_w(e, o):
-            raw = keep.tile([P, PACK, K], F32, name="w_raw", tag="w_raw%d%d" % (e, o))
+            raw = keep.tile([P, PACK, K], F32, name="w_raw", tag="w_raw%d%d" % (e % E, o))
             nc.sync.dma_start(raw[:], w[e, o * 512 : (o + 1) * 512, :].rearrange("(p j) k -> p j k", j=PACK))
             w_raw[e, o] = raw
 
         gates = {}
 
-        def load_gate(e):
-            g = keep.tile([P, C], F32, name="gate%d" % e)
+        def load_gate(e, tag):
+            g = keep.tile([P, C], F32, name="gate", tag=tag, align_bytes=64)
             nc.sync.dma_start(g[:], gate[0:P, e * C : (e + 1) * C])
             gates[e] = g
 
-        for e in range(E):
-            for o in range(PASSES):
-                load_w(e, o)
-        load_gate(0)
         for o in range(PASSES):
-            load_w(E, o)
-        load_gate(1)
-        for r in range(4):
-            nc.sync.dma_start(token_scales1[:].bitcast(I32)[r:P:32, :], scale_rows[r, :, 1, :])
+            load_w(0, o)
+        load_gate(0, "gate0")
+        for o in range(PASSES):
+            load_w(1, o)
+        move_scales(nc.sync, token_scales, scale_window)
 
-        slot_scales0 = keep.tile([P, S], U8, name="slot_scales0", align_bytes=64)
-        nc.vector.tensor_copy(slot_scales0[:], token_scales[:].indirect(offsets[:]))
-        for r in range(4):
-            nc.scalar.dma_start(
-                slot_scales1[:].bitcast(I32)[r:P:32, :], slot_scales0[:].bitcast(I32)[SHIFT + r : P : 32, :]
-            )
-        slot_scales = [slot_scales0, slot_scales1]
+        slot_scale_rows = keep.tile([P, S], U8, name="slot_scale_rows", align_bytes=64)
+        nc.vector.tensor_copy(slot_scale_rows[:], scale_window[:].indirect(offsets[:]))
+        move_scales(nc.scalar, slot_scales, slot_scale_rows)
         slot_words0 = keep.tile([P, S], U32, name="slot_words0", align_bytes=64)
         nc.vector.tensor_copy(slot_words0[:], token_words[0][:].bitcast(U32).indirect(offsets[:]))
         slot_words = {(0, e): slot_words0[:, e * C : (e + 1) * C] for e in range(E)}
@@ -129,31 +135,39 @@ def tile_moe_bds_lin_none_kernel(tc, dy_words, dy_scales, w, gate, offs, out):
                     stop=(o == PASSES - 1),
                 )
 
-        def routed(e, b, staged):
+        def routed(e, b, pieces):
             acc = psum.tile([P, C], F32, name="dx", tag="ring2", bufs=2)
             cols = slice(e * C, (e + 1) * C)
-            product(acc[:], e, b, [slot_words[o, e] for o in range(PASSES)], [s[:, cols] for s in slot_scales])
-            nc.scalar.copy(staged, acc[:])
-            nc.vector.tensor_tensor(windows[b][:].indirect(slot_offsets(e)), staged, gates[e][:], MULT)
+            product(acc[:], e, b, [slot_words[o, e] for o in range(PASSES)], [slot_scales[:, o, cols] for o in range(PASSES)])
+            lo = 0
+            for staged in pieces:
+                hi = lo + staged.shape[1]
+                nc.scalar.copy(staged, acc[:, lo:hi])
+                where = offsets[:, (e * C + lo) // 16 : (e * C + hi) // 16]
+                nc.vector.tensor_tensor(windows[b][:].indirect(where), staged, gates[e][:, lo:hi], MULT)
+                lo = hi
 
         def shared(acc, b, c):
             cols = slice(c * BANK, (c + 1) * BANK)
-            product(acc, E, b, [t[:, cols] for t in token_words], [token_scales[:, cols], token_scales1[:, cols]])
+            product(acc, E, b, [t[:, cols] for t in token_words], [token_scales[:, o, cols] for o in range(PASSES)])
 
         gather_pass1(0, "slot_words10")
         for o in range(PASSES):
             quantize_w(0, o)
+            load_w(E, o)
+        load_gate(1, "w_grouped00")
         gather_pass1(1, "w_grouped01")
         for o in range(PASSES):
             quantize_w(1, o)
+        staged_first = keep.tile([P, C // 2], F32, name="staged_first")
         staged_a = keep.tile([P, 2 * C], F32, name="staged_a", tag="w_raw11")
-        routed(0, 0, staged_a[:, 0:C])
+        routed(0, 0, [staged_first[:], staged_a[:, 0 : C // 2]])
         for o in range(PASSES):
             quantize_w(E, o)
-        staged_b = keep.tile([P, 2 * C], F32, name="staged_b", tag="w_raw21")
-        routed(1, 0, staged_b[:, 0:C])
-        routed(0, 1, staged_b[:, C : 2 * C])
-        routed(1, 1, staged_a[:, C : 2 * C])
+        staged_b = keep.tile([P, 2 * C], F32, name="staged_b", tag="w_raw01")
+        routed(1, 0, [staged_b[:, 0:C]])
+        routed(0, 1, [staged_b[:, C : 2 * C]])
+        routed(1, 1, [staged_a[:, C : 2 * C]])
 
         ds0 = keep.tile([P, T], F32, name="ds0")
         for c in range(T // BANK):
@@ -181,8 +195,10 @@ def tile_moe_bds_lin_none_kernel(tc, dy_words, dy_scales, w, gate, offs, out):
             nc.scalar.copy(result[:], back[:])
             nc.sync.dma_start(out[0:P, c * BANK : (c + 1) * BANK], result[:])
 
-        for c in range(T // BANK):
-            cols = slice(c * BANK, (c + 1) * BANK)
-            result = keep.tile([P, BANK], F32, name="result1_%d" % c)
-            nc.vector.tensor_tensor(result[:], ds1[c][:], windows[1][:, cols], ADD)
-            nc.sync.dma_start(out[P : 2 * P, cols], result[:])
+        lo = 0
+        for i, width in enumerate((512, 512, 256, 256)):
+            cols = slice(lo, lo + width)
+            result = keep.tile([P, width], F32, name="result1_%d" % i)
+            nc.vector.tensor_tensor(result[:], ds1[lo // BANK][:, lo % BANK : lo % BANK + width], windows[1][:, cols], ADD)
+            (nc.scalar, nc.sync)[i % 2].dma_start(out[P : 2 * P, cols], result[:])
+            lo = lo + width

@@ -40,7 +40,7 @@ def tile_moe_bds_lin_none_kernel(tc, dy_words, dy_scales, w, gate, offs, out):
         def slot_offsets(e):
             return offsets[:, e * (C // 16) : (e + 1) * (C // 16)]
 
-        scale_window = keep.tile([P, T], U8, name="scale_window", align_bytes=64)
+        scale_window = keep.tile([P, T], U8, name="scale_window", tag="scale_window", align_bytes=64)
         for q in range(QUADS):
             nc.sync.dma_start(
                 scale_window[:].bitcast(I32)[32 * q + FIRST : 32 * (q + 1), :],
@@ -57,7 +57,7 @@ def tile_moe_bds_lin_none_kernel(tc, dy_words, dy_scales, w, gate, offs, out):
         slot_scales = keep.tile([P, PASSES, S], U8, name="slot_scales", align_bytes=64)
         nc.vector.memset(slot_scales[:].bitcast(I32), 0)
         token_scales = keep.tile([P, PASSES, T], U8, name="token_scales", align_bytes=64)
-        nc.vector.memset(token_scales[:].bitcast(I32), 0)
+        nc.gpsimd.memset(token_scales[:].bitcast(I32), 0)
 
         def move_scales(queue, planes, rows):
             for o in range(PASSES):
@@ -65,7 +65,7 @@ def tile_moe_bds_lin_none_kernel(tc, dy_words, dy_scales, w, gate, offs, out):
                 queue.dma_start(planes[:].bitcast(I32)[0:MOVED, o, :], rows[:].bitcast(I32)[first : first + MOVED, :])
 
         windows = [keep.tile([P, T], F32, name="window%d" % b) for b in range(2)]
-        zeros = keep.tile([P, 64], F32, name="zeros")
+        zeros = keep.tile([P, 64], F32, name="zeros", tag="stage2")
         nc.gpsimd.memset(zeros[:], 0.0)
         for window in windows:
             nc.scalar.copy(
@@ -76,10 +76,12 @@ def tile_moe_bds_lin_none_kernel(tc, dy_words, dy_scales, w, gate, offs, out):
 
         w_raw = {}
 
-        def load_w(e, o):
-            raw = keep.tile([P, PACK, K], F32, name="w_raw", tag="w_raw%d%d" % (e % E, o))
-            nc.sync.dma_start(raw[:], w[e, o * 512 : (o + 1) * 512, :].rearrange("(p j) k -> p j k", j=PACK))
+        def load_w(e, o, raw):
+            nc.sync.dma_start(raw, w[e, o * 512 : (o + 1) * 512, :].rearrange("(p j) k -> p j k", j=PACK))
             w_raw[e, o] = raw
+
+        def pass_stage(o):
+            return keep.tile([P, PACK, K], F32, name="w_raw", tag="stage%d" % o)[:]
 
         gates = {}
 
@@ -89,23 +91,25 @@ def tile_moe_bds_lin_none_kernel(tc, dy_words, dy_scales, w, gate, offs, out):
             gates[e] = g
 
         for o in range(PASSES):
-            load_w(0, o)
+            load_w(0, o, pass_stage(o))
         load_gate(0, "gate0")
-        for o in range(PASSES):
-            load_w(1, o)
-        move_scales(nc.sync, token_scales, scale_window)
+        scale_rows = dy_scales.bitcast(I32).rearrange("o (q r) c -> r q o c", r=4)
+        for r in range(4):
+            nc.gpsimd.dma_start(token_scales[:].bitcast(I32)[r:P:32, :, :], scale_rows[r])
 
         slot_scale_rows = keep.tile([P, S], U8, name="slot_scale_rows", align_bytes=64)
         nc.vector.tensor_copy(slot_scale_rows[:], scale_window[:].indirect(offsets[:]))
-        move_scales(nc.scalar, slot_scales, slot_scale_rows)
-        slot_words0 = keep.tile([P, S], U32, name="slot_words0", align_bytes=64)
-        nc.vector.tensor_copy(slot_words0[:], token_words[0][:].bitcast(U32).indirect(offsets[:]))
-        slot_words = {(0, e): slot_words0[:, e * C : (e + 1) * C] for e in range(E)}
+        move_scales(nc.sync, slot_scales, slot_scale_rows)
+        w1_raw = keep.tile([P, PASSES, PACK, K], F32, name="w1_raw", tag="stage2")
+        for o in range(PASSES):
+            load_w(1, o, w1_raw[:, o, :, :])
+        early_words = keep.tile([P, S + C], U32, name="early_words", tag="scale_window", align_bytes=64)
+        nc.vector.tensor_copy(early_words[:, 0:S], token_words[0][:].bitcast(U32).indirect(offsets[:]))
+        slot_words = {(0, e): early_words[:, e * C : (e + 1) * C] for e in range(E)}
 
-        def gather_pass1(e, tag):
-            words = keep.tile([P, C], U32, name="slot_words1", tag=tag, align_bytes=64)
-            nc.vector.tensor_copy(words[:], token_words[1][:].bitcast(U32).indirect(slot_offsets(e)))
-            slot_words[1, e] = words[:]
+        def gather_pass1(e, words):
+            nc.vector.tensor_copy(words, token_words[1][:].bitcast(U32).indirect(slot_offsets(e)))
+            slot_words[1, e] = words
 
         codes = {}
         scales = {}
@@ -114,7 +118,7 @@ def tile_moe_bds_lin_none_kernel(tc, dy_words, dy_scales, w, gate, offs, out):
             grouped = keep.tile([P, K, PACK], BF16, name="w_grouped", tag="w_grouped%d%d" % (e, o), align_bytes=64)
             nc.scalar.copy(
                 grouped[:].rearrange("p (c i) j -> p c j i", i=4),
-                w_raw[e, o][:].rearrange("p j (c i) -> p c j i", i=4),
+                w_raw[e, o].rearrange("p j (c i) -> p c j i", i=4),
             )
             codes[e, o] = keep.tile([P, K], U32, name="w_codes%d%d" % (e, o), align_bytes=64)
             scales[e, o] = keep.tile([P, K], U8, name="w_scales%d%d" % (e, o), align_bytes=64)
@@ -151,20 +155,21 @@ def tile_moe_bds_lin_none_kernel(tc, dy_words, dy_scales, w, gate, offs, out):
             cols = slice(c * BANK, (c + 1) * BANK)
             product(acc, E, b, [t[:, cols] for t in token_words], [token_scales[:, o, cols] for o in range(PASSES)])
 
-        gather_pass1(0, "slot_words10")
+        gather_pass1(0, early_words[:, S : S + C])
         for o in range(PASSES):
             quantize_w(0, o)
-            load_w(E, o)
+            load_w(E, o, pass_stage(o))
         load_gate(1, "w_grouped00")
-        gather_pass1(1, "w_grouped01")
+        late_words = keep.tile([P, C], U32, name="late_words", tag="w_grouped01", align_bytes=64)
+        gather_pass1(1, late_words[:])
         for o in range(PASSES):
             quantize_w(1, o)
         staged_first = keep.tile([P, C // 2], F32, name="staged_first")
-        staged_a = keep.tile([P, 2 * C], F32, name="staged_a", tag="w_raw11")
+        staged_a = keep.tile([P, 2 * C], F32, name="staged_a", tag="stage2")
         routed(0, 0, [staged_first[:], staged_a[:, 0 : C // 2]])
         for o in range(PASSES):
             quantize_w(E, o)
-        staged_b = keep.tile([P, 2 * C], F32, name="staged_b", tag="w_raw01")
+        staged_b = keep.tile([P, 2 * C], F32, name="staged_b", tag="stage1")
         routed(1, 0, [staged_b[:, 0:C]])
         routed(0, 1, [staged_b[:, C : 2 * C]])
         routed(1, 1, [staged_a[:, C : 2 * C]])
@@ -200,5 +205,5 @@ def tile_moe_bds_lin_none_kernel(tc, dy_words, dy_scales, w, gate, offs, out):
             cols = slice(lo, lo + width)
             result = keep.tile([P, width], F32, name="result1_%d" % i)
             nc.vector.tensor_tensor(result[:], ds1[lo // BANK][:, lo % BANK : lo % BANK + width], windows[1][:, cols], ADD)
-            (nc.scalar, nc.sync)[i % 2].dma_start(out[P : 2 * P, cols], result[:])
+            nc.sync.dma_start(out[P : 2 * P, cols], result[:])
             lo = lo + width

@@ -48,16 +48,13 @@ def tile_moe_bds_lin_none_kernel(tc, dy_words, dy_scales, w, gate, offs, out):
             )
             nc.vector.memset(scale_window[:].bitcast(I32)[32 * q : 32 * q + FIRST, :], 0)
 
-        token_words = []
-        for o in range(PASSES):
-            words = keep.tile([P, T], I32, name="token_words%d" % o, align_bytes=64)
-            nc.sync.dma_start(words[:], dy_words[o].rearrange("p t d -> p (t d)").bitcast(I32))
-            token_words.append(words)
+        token_words = [keep.tile([P, T], I32, name="token_words%d" % o, align_bytes=64) for o in range(PASSES)]
+
+        def load_words(o):
+            nc.sync.dma_start(token_words[o][:], dy_words[o].rearrange("p t d -> p (t d)").bitcast(I32))
 
         slot_scales = keep.tile([P, PASSES, S], U8, name="slot_scales", align_bytes=64)
         nc.vector.memset(slot_scales[:].bitcast(I32), 0)
-        token_scales = keep.tile([P, PASSES, T], U8, name="token_scales", align_bytes=64)
-        nc.gpsimd.memset(token_scales[:].bitcast(I32), 0)
 
         def move_scales(queue, planes, rows):
             for o in range(PASSES):
@@ -73,6 +70,8 @@ def tile_moe_bds_lin_none_kernel(tc, dy_words, dy_scales, w, gate, offs, out):
             )
         ident = keep.tile([P, P], F32, name="ident")
         make_identity(nc, ident[:])
+        token_scales = keep.tile([P, PASSES, T], U8, name="token_scales", align_bytes=64)
+        nc.gpsimd.memset(token_scales[:].bitcast(I32), 0)
 
         w_raw = {}
 
@@ -83,19 +82,15 @@ def tile_moe_bds_lin_none_kernel(tc, dy_words, dy_scales, w, gate, offs, out):
         def pass_stage(o):
             return keep.tile([P, PACK, K], F32, name="w_raw", tag="stage%d" % o)[:]
 
-        gates = {}
-
-        def load_gate(e, tag):
-            g = keep.tile([P, C], F32, name="gate", tag=tag, align_bytes=64)
-            nc.sync.dma_start(g[:], gate[0:P, e * C : (e + 1) * C])
-            gates[e] = g
-
+        load_words(0)
+        gate_cols = keep.tile([P, E, PACK], F32, name="gate_cols")
+        nc.sync.dma_start(gate_cols[:], gate[0, :].rearrange("(e p a) -> p e a", e=E, a=PACK))
         for o in range(PASSES):
             load_w(0, o, pass_stage(o))
-        load_gate(0, "gate0")
+        load_words(1)
         scale_rows = dy_scales.bitcast(I32).rearrange("o (q r) c -> r q o c", r=4)
         for r in range(4):
-            nc.gpsimd.dma_start(token_scales[:].bitcast(I32)[r:P:32, :, :], scale_rows[r])
+            nc.sync.dma_start(token_scales[:].bitcast(I32)[r:P:32, :, :], scale_rows[r])
 
         slot_scale_rows = keep.tile([P, S], U8, name="slot_scale_rows", align_bytes=64)
         nc.vector.tensor_copy(slot_scale_rows[:], scale_window[:].indirect(offsets[:]))
@@ -139,40 +134,53 @@ def tile_moe_bds_lin_none_kernel(tc, dy_words, dy_scales, w, gate, offs, out):
                     stop=(o == PASSES - 1),
                 )
 
-        def routed(e, b, pieces):
+        def routed(e, b):
             acc = psum.tile([P, C], F32, name="dx", tag="ring2", bufs=2)
             cols = slice(e * C, (e + 1) * C)
             product(acc[:], e, b, [slot_words[o, e] for o in range(PASSES)], [slot_scales[:, o, cols] for o in range(PASSES)])
-            lo = 0
-            for staged in pieces:
-                hi = lo + staged.shape[1]
-                nc.scalar.copy(staged, acc[:, lo:hi])
-                where = offsets[:, (e * C + lo) // 16 : (e * C + hi) // 16]
-                nc.vector.tensor_tensor(windows[b][:].indirect(where), staged, gates[e][:, lo:hi], MULT)
-                lo = hi
+            return acc
+
+        def scatter(b, first, staged):
+            last = first + staged.shape[1]
+            where = offsets[:, first // 16 : last // 16]
+            nc.vector.tensor_tensor(windows[b][:].indirect(where), staged, gates[:, first:last], MULT)
 
         def shared(acc, b, c):
             cols = slice(c * BANK, (c + 1) * BANK)
             product(acc, E, b, [t[:, cols] for t in token_words], [token_scales[:, o, cols] for o in range(PASSES)])
 
-        gather_pass1(0, early_words[:, S : S + C])
         for o in range(PASSES):
             quantize_w(0, o)
             load_w(E, o, pass_stage(o))
-        load_gate(1, "w_grouped00")
+        gather_pass1(0, early_words[:, S : S + C])
         late_words = keep.tile([P, C], U32, name="late_words", tag="w_grouped01", align_bytes=64)
         gather_pass1(1, late_words[:])
+
+        gates = keep.tile([P, S], F32, name="gates")
+        for e in range(E):
+            spread = psum.tile([P, PACK, P], F32, name="spread", tag="ring3", bufs=3)
+            for a in range(PACK):
+                nc.tensor.transpose(spread[:, a, :], gate_cols[:, e, a : a + 1].to_broadcast([P, P]), ident[:])
+            nc.scalar.copy(
+                gates[:, e * C : (e + 1) * C].rearrange("m (p a) -> m p a", a=PACK), spread[:].rearrange("m a p -> m p a")
+            )
+
+        acc = routed(0, 0)
+        staged_first = keep.tile([P, C // 2], F32, name="staged_first")
+        nc.scalar.copy(staged_first[:], acc[:, 0 : C // 2])
+        scatter(0, 0, staged_first[:])
         for o in range(PASSES):
             quantize_w(1, o)
-        staged_first = keep.tile([P, C // 2], F32, name="staged_first")
-        staged_a = keep.tile([P, 2 * C], F32, name="staged_a", tag="stage2")
-        routed(0, 0, [staged_first[:], staged_a[:, 0 : C // 2]])
+        staged_a = keep.tile([P, C // 2], F32, name="staged_a", tag="stage2")
+        nc.scalar.copy(staged_a[:], acc[:, C // 2 : C])
+        scatter(0, C // 2, staged_a[:])
         for o in range(PASSES):
             quantize_w(E, o)
-        staged_b = keep.tile([P, 2 * C], F32, name="staged_b", tag="stage1")
-        routed(1, 0, [staged_b[:, 0:C]])
-        routed(0, 1, [staged_b[:, C : 2 * C]])
-        routed(1, 1, [staged_a[:, C : 2 * C]])
+        staged_b = keep.tile([P, 3 * C], F32, name="staged_b", tag="stage1")
+        for i, (e, b) in enumerate(((1, 0), (0, 1), (1, 1))):
+            nc.scalar.copy(staged_b[:, i * C : (i + 1) * C], routed(e, b)[:])
+        scatter(0, C, staged_b[:, 0:C])
+        scatter(1, 0, staged_b[:, C : 3 * C])
 
         ds0 = keep.tile([P, T], F32, name="ds0")
         for c in range(T // BANK):

@@ -5,16 +5,23 @@ from concourse.masks import make_identity
 
 K, T, E, C, N = 256, 1536, 2, 512, 1024
 S = E * C
+SHARED = E
 P = 128
 PACK = 4
 PASSES = N // (P * PACK)
 BANK = 512
-QUADS = 4
-FIRST = 24
-MOVED = 100
+QUADRANT = 32
+LIVE = 4
+FIRST_ROW = QUADRANT - PASSES * LIVE
+MOVED_ROWS = P - QUADRANT + LIVE
+PER_COLUMN = 16
+LINE = 4
+HALF = C // 2
+ZEROS = 64
+LAST_WIDTHS = (512, 512, 256, 256)
 
 FLOPS = 2 * N * K * (S + T)
-BYTES = N * T + N * T // 32 + 4 * (E + 1) * N * K + 4 * S + 2 * P * (S // 16) + 4 * K * T
+BYTES = N * T + N * T // 32 + 4 * (E + 1) * N * K + 4 * S + 2 * P * (S // PER_COLUMN) + 4 * K * T
 
 F32 = mybir.dt.float32
 BF16 = mybir.dt.bfloat16
@@ -34,49 +41,46 @@ def tile_moe_bds_lin_none_kernel(tc, dy_words, dy_scales, w, gate, offs, out):
         keep = ctx.enter_context(tc.tile_pool(name="keep", bufs=1))
         psum = ctx.enter_context(tc.psum_pool(name="psum", bufs=1))
 
-        offsets = keep.tile([P, S // 16], U16, name="offsets")
+        offsets = keep.tile([P, S // PER_COLUMN], U16, name="offsets")
         nc.sync.dma_start(offsets[:], offs)
 
-        def slot_offsets(e):
-            return offsets[:, e * (C // 16) : (e + 1) * (C // 16)]
+        def entries(first, last):
+            return offsets[:, first // PER_COLUMN : last // PER_COLUMN]
 
         scale_window = keep.tile([P, T], U8, name="scale_window", tag="scale_window", align_bytes=64)
-        for q in range(QUADS):
+        for q in range(P // QUADRANT):
             nc.sync.dma_start(
-                scale_window[:].bitcast(I32)[32 * q + FIRST : 32 * (q + 1), :],
-                dy_scales.bitcast(I32)[:, 4 * q : 4 * (q + 1), :],
+                scale_window[:].bitcast(I32)[QUADRANT * q + FIRST_ROW : QUADRANT * (q + 1), :],
+                dy_scales.bitcast(I32)[:, LIVE * q : LIVE * (q + 1), :],
             )
-            nc.vector.memset(scale_window[:].bitcast(I32)[32 * q : 32 * q + FIRST, :], 0)
+            nc.vector.memset(scale_window[:].bitcast(I32)[QUADRANT * q : QUADRANT * q + FIRST_ROW, :], 0)
 
         token_words = [keep.tile([P, T], I32, name="token_words%d" % o, align_bytes=64) for o in range(PASSES)]
 
         def load_words(o):
             nc.sync.dma_start(token_words[o][:], dy_words[o].rearrange("p t d -> p (t d)").bitcast(I32))
 
-        slot_scales = keep.tile([P, PASSES, S], U8, name="slot_scales", align_bytes=64)
-        nc.vector.memset(slot_scales[:].bitcast(I32), 0)
+        slot_planes = keep.tile([P, PASSES, S], U8, name="slot_planes", align_bytes=64)
+        nc.vector.memset(slot_planes[:].bitcast(I32), 0)
 
-        def move_scales(queue, planes, rows):
-            for o in range(PASSES):
-                first = FIRST + 4 * o
-                queue.dma_start(planes[:].bitcast(I32)[0:MOVED, o, :], rows[:].bitcast(I32)[first : first + MOVED, :])
-
-        windows = [keep.tile([P, T], F32, name="window%d" % b) for b in range(2)]
-        zeros = keep.tile([P, 64], F32, name="zeros", tag="stage2")
+        windows = [keep.tile([P, T], F32, name="window%d" % b) for b in range(K // P)]
+        zeros = keep.tile([P, ZEROS], F32, name="zeros", tag="stage2")
         nc.gpsimd.memset(zeros[:], 0.0)
         for window in windows:
             nc.scalar.copy(
-                window[:].rearrange("p (a b) -> p a b", b=64), zeros[:].unsqueeze(1).to_broadcast([P, T // 64, 64])
+                window[:].rearrange("p (a b) -> p a b", b=ZEROS),
+                zeros[:].unsqueeze(1).to_broadcast([P, T // ZEROS, ZEROS]),
             )
         ident = keep.tile([P, P], F32, name="ident")
         make_identity(nc, ident[:])
-        token_scales = keep.tile([P, PASSES, T], U8, name="token_scales", align_bytes=64)
-        nc.gpsimd.memset(token_scales[:].bitcast(I32), 0)
+        token_planes = keep.tile([P, PASSES, T], U8, name="token_planes", align_bytes=64)
+        nc.gpsimd.memset(token_planes[:].bitcast(I32), 0)
 
         w_raw = {}
 
         def load_w(e, o, raw):
-            nc.sync.dma_start(raw, w[e, o * 512 : (o + 1) * 512, :].rearrange("(p j) k -> p j k", j=PACK))
+            rows = slice(o * P * PACK, (o + 1) * P * PACK)
+            nc.sync.dma_start(raw, w[e, rows, :].rearrange("(p j) k -> p j k", j=PACK))
             w_raw[e, o] = raw
 
         def pass_stage(o):
@@ -88,103 +92,118 @@ def tile_moe_bds_lin_none_kernel(tc, dy_words, dy_scales, w, gate, offs, out):
         for o in range(PASSES):
             load_w(0, o, pass_stage(o))
         load_words(1)
-        scale_rows = dy_scales.bitcast(I32).rearrange("o (q r) c -> r q o c", r=4)
-        for r in range(4):
-            nc.sync.dma_start(token_scales[:].bitcast(I32)[r:P:32, :, :], scale_rows[r])
+        scale_rows = dy_scales.bitcast(I32).rearrange("o (q r) c -> r q o c", r=LIVE)
+        for r in range(LIVE):
+            nc.sync.dma_start(token_planes[:].bitcast(I32)[r:P:QUADRANT, :, :], scale_rows[r])
 
         slot_scale_rows = keep.tile([P, S], U8, name="slot_scale_rows", align_bytes=64)
         nc.vector.tensor_copy(slot_scale_rows[:], scale_window[:].indirect(offsets[:]))
-        move_scales(nc.sync, slot_scales, slot_scale_rows)
+        for o in range(PASSES):
+            first = FIRST_ROW + LIVE * o
+            nc.sync.dma_start(
+                slot_planes[:].bitcast(I32)[0:MOVED_ROWS, o, :],
+                slot_scale_rows[:].bitcast(I32)[first : first + MOVED_ROWS, :],
+            )
         w1_raw = keep.tile([P, PASSES, PACK, K], F32, name="w1_raw", tag="stage2")
         for o in range(PASSES):
             load_w(1, o, w1_raw[:, o, :, :])
+
         early_words = keep.tile([P, S + C], U32, name="early_words", tag="scale_window", align_bytes=64)
         nc.vector.tensor_copy(early_words[:, 0:S], token_words[0][:].bitcast(U32).indirect(offsets[:]))
         slot_words = {(0, e): early_words[:, e * C : (e + 1) * C] for e in range(E)}
 
         def gather_pass1(e, words):
-            nc.vector.tensor_copy(words, token_words[1][:].bitcast(U32).indirect(slot_offsets(e)))
+            nc.vector.tensor_copy(words, token_words[1][:].bitcast(U32).indirect(entries(e * C, (e + 1) * C)))
             slot_words[1, e] = words
 
-        codes = {}
-        scales = {}
+        w_codes = {}
+        w_planes = {}
 
-        def quantize_w(e, o):
-            grouped = keep.tile([P, K, PACK], BF16, name="w_grouped", tag="w_grouped%d%d" % (e, o), align_bytes=64)
+        def quantize_w(e, o, tag):
+            grouped = keep.tile([P, K, PACK], BF16, name="w_grouped", tag=tag, align_bytes=64)
             nc.scalar.copy(
-                grouped[:].rearrange("p (c i) j -> p c j i", i=4),
-                w_raw[e, o].rearrange("p j (c i) -> p c j i", i=4),
+                grouped[:].rearrange("p (c i) j -> p c j i", i=LINE),
+                w_raw[e, o].rearrange("p j (c i) -> p c j i", i=LINE),
             )
-            codes[e, o] = keep.tile([P, K], U32, name="w_codes%d%d" % (e, o), align_bytes=64)
-            scales[e, o] = keep.tile([P, K], U8, name="w_scales%d%d" % (e, o), align_bytes=64)
+            w_codes[e, o] = keep.tile([P, K], U32, name="w_codes%d%d" % (e, o), align_bytes=64)
+            w_planes[e, o] = keep.tile([P, K], U8, name="w_planes%d%d" % (e, o), align_bytes=64)
             nc.vector.quantize_mx(
-                out=codes[e, o][:].bitcast(E4M3), scales=scales[e, o][:], in_=grouped[:].rearrange("p k j -> p (k j)")
+                out=w_codes[e, o][:].bitcast(E4M3),
+                scales=w_planes[e, o][:],
+                in_=grouped[:].rearrange("p k j -> p (k j)"),
             )
 
-        def product(acc, e, b, moving, moving_scales):
-            cols = slice(b * P, (b + 1) * P)
+        def product(acc, e, b, words, planes):
+            rows = slice(b * P, (b + 1) * P)
             for o in range(PASSES):
                 nc.tensor.matmul_mx(
                     out=acc,
-                    lhsT=codes[e, o][:, cols].bitcast(E4M3),
-                    lhsT_scale=scales[e, o][:, cols],
-                    rhs=moving[o].bitcast(E5M2),
-                    rhs_scale=moving_scales[o],
+                    lhsT=w_codes[e, o][:, rows].bitcast(E4M3),
+                    lhsT_scale=w_planes[e, o][:, rows],
+                    rhs=words[o].bitcast(E5M2),
+                    rhs_scale=planes[o],
                     start=(o == 0),
                     stop=(o == PASSES - 1),
                 )
 
         def routed(e, b):
-            acc = psum.tile([P, C], F32, name="dx", tag="ring2", bufs=2)
-            cols = slice(e * C, (e + 1) * C)
-            product(acc[:], e, b, [slot_words[o, e] for o in range(PASSES)], [slot_scales[:, o, cols] for o in range(PASSES)])
+            acc = psum.tile([P, C], F32, name="dx", tag="two_banks", bufs=2)
+            slots = slice(e * C, (e + 1) * C)
+            words = [slot_words[o, e] for o in range(PASSES)]
+            product(acc[:], e, b, words, [slot_planes[:, o, slots] for o in range(PASSES)])
             return acc
 
         def scatter(b, first, staged):
             last = first + staged.shape[1]
-            where = offsets[:, first // 16 : last // 16]
-            nc.vector.tensor_tensor(windows[b][:].indirect(where), staged, gates[:, first:last], MULT)
+            nc.vector.tensor_tensor(windows[b][:].indirect(entries(first, last)), staged, gates[:, first:last], MULT)
 
         def shared(acc, b, c):
-            cols = slice(c * BANK, (c + 1) * BANK)
-            product(acc, E, b, [t[:, cols] for t in token_words], [token_scales[:, o, cols] for o in range(PASSES)])
+            tokens = slice(c * BANK, (c + 1) * BANK)
+            words = [token_words[o][:, tokens] for o in range(PASSES)]
+            product(acc, SHARED, b, words, [token_planes[:, o, tokens] for o in range(PASSES)])
 
         for o in range(PASSES):
-            quantize_w(0, o)
-            load_w(E, o, pass_stage(o))
+            quantize_w(0, o, "w_grouped0%d" % o)
+            load_w(SHARED, o, pass_stage(o))
         gather_pass1(0, early_words[:, S : S + C])
         late_words = keep.tile([P, C], U32, name="late_words", tag="w_grouped01", align_bytes=64)
         gather_pass1(1, late_words[:])
 
         gates = keep.tile([P, S], F32, name="gates")
         for e in range(E):
-            spread = psum.tile([P, PACK, P], F32, name="spread", tag="ring3", bufs=3)
+            spread = psum.tile([P, PACK, P], F32, name="spread", tag="three_banks", bufs=3)
             for a in range(PACK):
                 nc.tensor.transpose(spread[:, a, :], gate_cols[:, e, a : a + 1].to_broadcast([P, P]), ident[:])
             nc.scalar.copy(
-                gates[:, e * C : (e + 1) * C].rearrange("m (p a) -> m p a", a=PACK), spread[:].rearrange("m a p -> m p a")
+                gates[:, e * C : (e + 1) * C].rearrange("m (p a) -> m p a", a=PACK),
+                spread[:].rearrange("m a p -> m p a"),
             )
 
         acc = routed(0, 0)
-        staged_first = keep.tile([P, C // 2], F32, name="staged_first")
-        nc.scalar.copy(staged_first[:], acc[:, 0 : C // 2])
+        staged_first = keep.tile([P, HALF], F32, name="staged_first")
+        nc.scalar.copy(staged_first[:], acc[:, 0:HALF])
         scatter(0, 0, staged_first[:])
         for o in range(PASSES):
-            quantize_w(1, o)
-        staged_a = keep.tile([P, C // 2], F32, name="staged_a", tag="stage2")
-        nc.scalar.copy(staged_a[:], acc[:, C // 2 : C])
-        scatter(0, C // 2, staged_a[:])
+            quantize_w(1, o, "w_grouped1%d" % o)
+        staged_second = keep.tile([P, HALF], F32, name="staged_second", tag="stage2")
+        nc.scalar.copy(staged_second[:], acc[:, HALF:C])
+        scatter(0, HALF, staged_second[:])
+        acc = routed(1, 0)
+        staged_third = keep.tile([P, HALF], F32, name="staged_third")
+        nc.scalar.copy(staged_third[:], acc[:, 0:HALF])
+        scatter(0, C, staged_third[:])
         for o in range(PASSES):
-            quantize_w(E, o)
-        staged_b = keep.tile([P, 3 * C], F32, name="staged_b", tag="stage1")
-        for i, (e, b) in enumerate(((1, 0), (0, 1), (1, 1))):
-            nc.scalar.copy(staged_b[:, i * C : (i + 1) * C], routed(e, b)[:])
-        scatter(0, C, staged_b[:, 0:C])
-        scatter(1, 0, staged_b[:, C : 3 * C])
+            quantize_w(SHARED, o, "w_grouped11")
+        staged_rest = keep.tile([P, HALF + S], F32, name="staged_rest", tag="stage1")
+        nc.scalar.copy(staged_rest[:, 0:HALF], acc[:, HALF:C])
+        scatter(0, C + HALF, staged_rest[:, 0:HALF])
+        for e in range(E):
+            nc.scalar.copy(staged_rest[:, HALF + e * C : HALF + (e + 1) * C], routed(e, 1)[:])
+        scatter(1, 0, staged_rest[:, HALF:])
 
         ds0 = keep.tile([P, T], F32, name="ds0")
         for c in range(T // BANK):
-            acc = psum.tile([P, BANK], F32, name="ds0_acc", tag="ring3", bufs=3)
+            acc = psum.tile([P, BANK], F32, name="ds0_acc", tag="three_banks", bufs=3)
             shared(acc[:], 0, c)
             nc.scalar.copy(ds0[:, c * BANK : (c + 1) * BANK], acc[:])
         ds1 = []
@@ -193,25 +212,26 @@ def tile_moe_bds_lin_none_kernel(tc, dy_words, dy_scales, w, gate, offs, out):
             shared(acc[:], 1, c)
             ds1.append(acc)
         for c in range(T // BANK):
-            turned = psum.tile([P, BANK], F32, name="turned", tag="ring3", bufs=3)
+            turned = psum.tile([P, BANK], F32, name="turned", tag="three_banks", bufs=3)
             for j in range(BANK // P):
-                cols = slice(c * BANK + j * P, c * BANK + (j + 1) * P)
-                dst = turned[:, j * P : (j + 1) * P]
-                nc.tensor.matmul(dst, ds0[:, cols], ident[:], start=True, stop=False, is_transpose=True)
-                nc.tensor.matmul(dst, windows[0][:, cols], ident[:], start=False, stop=True, is_transpose=True)
+                tokens = slice(c * BANK + j * P, c * BANK + (j + 1) * P)
+                block = turned[:, j * P : (j + 1) * P]
+                nc.tensor.matmul(block, ds0[:, tokens], ident[:], start=True, stop=False, is_transpose=True)
+                nc.tensor.matmul(block, windows[0][:, tokens], ident[:], start=False, stop=True, is_transpose=True)
             sums = keep.tile([P, BANK], F32, name="sums%d" % c)
             nc.scalar.copy(sums[:], turned[:])
-            back = psum.tile([P, BANK], F32, name="back", tag="ring2", bufs=2)
+            back = psum.tile([P, BANK], F32, name="back", tag="two_banks", bufs=2)
             for j in range(BANK // P):
                 nc.tensor.transpose(back[:, j * P : (j + 1) * P], sums[:, j * P : (j + 1) * P], ident[:])
             result = keep.tile([P, BANK], F32, name="result0_%d" % c)
             nc.scalar.copy(result[:], back[:])
-            nc.sync.dma_start(out[0:P, c * BANK : (c + 1) * BANK], result[:])
+            nc.scalar.dma_start(out[0:P, c * BANK : (c + 1) * BANK], result[:])
 
         lo = 0
-        for i, width in enumerate((512, 512, 256, 256)):
-            cols = slice(lo, lo + width)
+        for i, width in enumerate(LAST_WIDTHS):
+            tokens = slice(lo, lo + width)
             result = keep.tile([P, width], F32, name="result1_%d" % i)
-            nc.vector.tensor_tensor(result[:], ds1[lo // BANK][:, lo % BANK : lo % BANK + width], windows[1][:, cols], ADD)
-            nc.sync.dma_start(out[P : 2 * P, cols], result[:])
+            ds = ds1[lo // BANK][:, lo % BANK : lo % BANK + width]
+            nc.vector.tensor_tensor(result[:], ds, windows[1][:, tokens], ADD)
+            nc.sync.dma_start(out[P : 2 * P, tokens], result[:])
             lo = lo + width

from contextlib import ExitStack

import concourse.mybir as mybir
from concourse.masks import make_identity

K, T, E, C, N = 256, 1536, 2, 512, 1024
S = E * C
SHARED = E
P = 128
PACK = 4
PASSES = N // (P * PACK)
BANK = 512
QUADRANT = 32
LIVE = 4
FIRST_ROW = QUADRANT - PASSES * LIVE
MOVED_ROWS = P - QUADRANT + LIVE
PER_COLUMN = 16
LINE = 4
HALF = C // 2
ZEROS = 64
LAST_WIDTHS = (512, 512, 256, 256)

FLOPS = 2 * N * K * (S + T)
BYTES = N * T + N * T // 32 + 4 * (E + 1) * N * K + 4 * S + 2 * P * (S // PER_COLUMN) + 4 * K * T

F32 = mybir.dt.float32
BF16 = mybir.dt.bfloat16
I32 = mybir.dt.int32
U32 = mybir.dt.uint32
U16 = mybir.dt.uint16
U8 = mybir.dt.uint8
E4M3 = mybir.dt.float8_e4m3fn_x4
E5M2 = mybir.dt.float8_e5m2_x4
MULT = mybir.AluOpType.mult
ADD = mybir.AluOpType.add


def tile_moe_bds_lin_none_kernel(tc, dy_words, dy_scales, w, gate, offs, out):
    nc = tc.nc
    with ExitStack() as ctx:
        keep = ctx.enter_context(tc.tile_pool(name="keep", bufs=1))
        psum = ctx.enter_context(tc.psum_pool(name="psum", bufs=1))

        offsets = keep.tile([P, S // PER_COLUMN], U16, name="offsets")
        nc.sync.dma_start(offsets[:], offs)

        def entries(first, last):
            return offsets[:, first // PER_COLUMN : last // PER_COLUMN]

        scale_window = keep.tile([P, T], U8, name="scale_window", tag="scale_window", align_bytes=64)
        for q in range(P // QUADRANT):
            nc.sync.dma_start(
                scale_window[:].bitcast(I32)[QUADRANT * q + FIRST_ROW : QUADRANT * (q + 1), :],
                dy_scales.bitcast(I32)[:, LIVE * q : LIVE * (q + 1), :],
            )
            nc.vector.memset(scale_window[:].bitcast(I32)[QUADRANT * q : QUADRANT * q + FIRST_ROW, :], 0)

        token_words = [keep.tile([P, T], I32, name="token_words%d" % o, align_bytes=64) for o in range(PASSES)]

        def load_words(o):
            nc.sync.dma_start(token_words[o][:], dy_words[o].rearrange("p t d -> p (t d)").bitcast(I32))

        slot_planes = keep.tile([P, PASSES, S], U8, name="slot_planes", align_bytes=64)
        nc.vector.memset(slot_planes[:].bitcast(I32), 0)

        windows = [keep.tile([P, T], F32, name="window%d" % b) for b in range(K // P)]
        zeros = keep.tile([P, ZEROS], F32, name="zeros", tag="stage2")
        nc.gpsimd.memset(zeros[:], 0.0)
        for window in windows:
            nc.scalar.copy(
                window[:].rearrange("p (a b) -> p a b", b=ZEROS),
                zeros[:].unsqueeze(1).to_broadcast([P, T // ZEROS, ZEROS]),
            )
        ident = keep.tile([P, P], F32, name="ident")
        make_identity(nc, ident[:])
        token_planes = keep.tile([P, PASSES, T], U8, name="token_planes", align_bytes=64)
        nc.gpsimd.memset(token_planes[:].bitcast(I32), 0)

        w_raw = {}

        def load_w(e, o, raw):
            rows = slice(o * P * PACK, (o + 1) * P * PACK)
            nc.sync.dma_start(raw, w[e, rows, :].rearrange("(p j) k -> p j k", j=PACK))
            w_raw[e, o] = raw

        def pass_stage(o):
            return keep.tile([P, PACK, K], F32, name="w_raw", tag="stage%d" % o)[:]

        load_words(0)
        gate_cols = keep.tile([P, E, PACK], F32, name="gate_cols")
        nc.sync.dma_start(gate_cols[:], gate[0, :].rearrange("(e p a) -> p e a", e=E, a=PACK))
        for o in range(PASSES):
            load_w(0, o, pass_stage(o))
        load_words(1)
        scale_rows = dy_scales.bitcast(I32).rearrange("o (q r) c -> r q o c", r=LIVE)
        for r in range(LIVE):
            nc.sync.dma_start(token_planes[:].bitcast(I32)[r:P:QUADRANT, :, :], scale_rows[r])

        slot_scale_rows = keep.tile([P, S], U8, name="slot_scale_rows", align_bytes=64)
        nc.vector.tensor_copy(slot_scale_rows[:], scale_window[:].indirect(offsets[:]))
        for o in range(PASSES):
            first = FIRST_ROW + LIVE * o
            nc.sync.dma_start(
                slot_planes[:].bitcast(I32)[0:MOVED_ROWS, o, :],
                slot_scale_rows[:].bitcast(I32)[first : first + MOVED_ROWS, :],
            )
        w1_raw = keep.tile([P, PASSES, PACK, K], F32, name="w1_raw", tag="stage2")
        for o in range(PASSES):
            load_w(1, o, w1_raw[:, o, :, :])

        early_words = keep.tile([P, S + C], U32, name="early_words", tag="scale_window", align_bytes=64)
        nc.vector.tensor_copy(early_words[:, 0:S], token_words[0][:].bitcast(U32).indirect(offsets[:]))
        slot_words = {(0, e): early_words[:, e * C : (e + 1) * C] for e in range(E)}

        def gather_pass1(e, words):
            nc.vector.tensor_copy(words, token_words[1][:].bitcast(U32).indirect(entries(e * C, (e + 1) * C)))
            slot_words[1, e] = words

        w_codes = {}
        w_planes = {}

        def quantize_w(e, o, tag):
            grouped = keep.tile([P, K, PACK], BF16, name="w_grouped", tag=tag, align_bytes=64)
            nc.scalar.copy(
                grouped[:].rearrange("p (c i) j -> p c j i", i=LINE),
                w_raw[e, o].rearrange("p j (c i) -> p c j i", i=LINE),
            )
            w_codes[e, o] = keep.tile([P, K], U32, name="w_codes%d%d" % (e, o), align_bytes=64)
            w_planes[e, o] = keep.tile([P, K], U8, name="w_planes%d%d" % (e, o), align_bytes=64)
            nc.vector.quantize_mx(
                out=w_codes[e, o][:].bitcast(E4M3),
                scales=w_planes[e, o][:],
                in_=grouped[:].rearrange("p k j -> p (k j)"),
            )

        def product(acc, e, b, words, planes):
            rows = slice(b * P, (b + 1) * P)
            for o in range(PASSES):
                nc.tensor.matmul_mx(
                    out=acc,
                    lhsT=w_codes[e, o][:, rows].bitcast(E4M3),
                    lhsT_scale=w_planes[e, o][:, rows],
                    rhs=words[o].bitcast(E5M2),
                    rhs_scale=planes[o],
                    start=(o == 0),
                    stop=(o == PASSES - 1),
                )

        def routed(e, b):
            acc = psum.tile([P, C], F32, name="dx", tag="two_banks", bufs=2)
            slots = slice(e * C, (e + 1) * C)
            words = [slot_words[o, e] for o in range(PASSES)]
            product(acc[:], e, b, words, [slot_planes[:, o, slots] for o in range(PASSES)])
            return acc

        def scatter(b, first, staged):
            last = first + staged.shape[1]
            nc.vector.tensor_tensor(windows[b][:].indirect(entries(first, last)), staged, gates[:, first:last], MULT)

        def shared(acc, b, c):
            tokens = slice(c * BANK, (c + 1) * BANK)
            words = [token_words[o][:, tokens] for o in range(PASSES)]
            product(acc, SHARED, b, words, [token_planes[:, o, tokens] for o in range(PASSES)])

        for o in range(PASSES):
            quantize_w(0, o, "w_grouped0%d" % o)
            load_w(SHARED, o, pass_stage(o))
        gather_pass1(0, early_words[:, S : S + C])
        late_words = keep.tile([P, C], U32, name="late_words", tag="w_grouped01", align_bytes=64)
        gather_pass1(1, late_words[:])

        gates = keep.tile([P, S], F32, name="gates")
        for e in range(E):
            spread = psum.tile([P, PACK, P], F32, name="spread", tag="three_banks", bufs=3)
            for a in range(PACK):
                nc.tensor.transpose(spread[:, a, :], gate_cols[:, e, a : a + 1].to_broadcast([P, P]), ident[:])
            nc.scalar.copy(
                gates[:, e * C : (e + 1) * C].rearrange("m (p a) -> m p a", a=PACK),
                spread[:].rearrange("m a p -> m p a"),
            )

        acc = routed(0, 0)
        staged_first = keep.tile([P, HALF], F32, name="staged_first")
        nc.scalar.copy(staged_first[:], acc[:, 0:HALF])
        scatter(0, 0, staged_first[:])
        for o in range(PASSES):
            quantize_w(1, o, "w_grouped1%d" % o)
        staged_second = keep.tile([P, HALF], F32, name="staged_second", tag="stage2")
        nc.scalar.copy(staged_second[:], acc[:, HALF:C])
        scatter(0, HALF, staged_second[:])
        acc = routed(1, 0)
        staged_third = keep.tile([P, HALF], F32, name="staged_third")
        nc.scalar.copy(staged_third[:], acc[:, 0:HALF])
        scatter(0, C, staged_third[:])
        for o in range(PASSES):
            quantize_w(SHARED, o, "w_grouped11")
        staged_rest = keep.tile([P, HALF + S], F32, name="staged_rest", tag="stage1")
        nc.scalar.copy(staged_rest[:, 0:HALF], acc[:, HALF:C])
        scatter(0, C + HALF, staged_rest[:, 0:HALF])
        for e in range(E):
            nc.scalar.copy(staged_rest[:, HALF + e * C : HALF + (e + 1) * C], routed(e, 1)[:])
        scatter(1, 0, staged_rest[:, HALF:])

        ds0 = keep.tile([P, T], F32, name="ds0")
        for c in range(T // BANK):
            acc = psum.tile([P, BANK], F32, name="ds0_acc", tag="three_banks", bufs=3)
            shared(acc[:], 0, c)
            nc.scalar.copy(ds0[:, c * BANK : (c + 1) * BANK], acc[:])
        ds1 = []
        for c in range(T // BANK):
            acc = psum.tile([P, BANK], F32, name="ds1_acc%d" % c)
            shared(acc[:], 1, c)
            ds1.append(acc)
        for c in range(T // BANK):
            turned = psum.tile([P, BANK], F32, name="turned", tag="three_banks", bufs=3)
            for j in range(BANK // P):
                tokens = slice(c * BANK + j * P, c * BANK + (j + 1) * P)
                block = turned[:, j * P : (j + 1) * P]
                nc.tensor.matmul(block, ds0[:, tokens], ident[:], start=True, stop=False, is_transpose=True)
                nc.tensor.matmul(block, windows[0][:, tokens], ident[:], start=False, stop=True, is_transpose=True)
            sums = keep.tile([P, BANK], F32, name="sums%d" % c)
            nc.scalar.copy(sums[:], turned[:])
            back = psum.tile([P, BANK], F32, name="back", tag="two_banks", bufs=2)
            for j in range(BANK // P):
                nc.tensor.transpose(back[:, j * P : (j + 1) * P], sums[:, j * P : (j + 1) * P], ident[:])
            result = keep.tile([P, BANK], F32, name="result0_%d" % c)
            nc.scalar.copy(result[:], back[:])
            nc.scalar.dma_start(out[0:P, c * BANK : (c + 1) * BANK], result[:])

        lo = 0
        for i, width in enumerate(LAST_WIDTHS):
            tokens = slice(lo, lo + width)
            result = keep.tile([P, width], F32, name="result1_%d" % i)
            ds = ds1[lo // BANK][:, lo % BANK : lo % BANK + width]
            nc.vector.tensor_tensor(result[:], ds, windows[1][:, tokens], ADD)
            nc.sync.dma_start(out[P : 2 * P, tokens], result[:])
            lo = lo + width
